import numpy as np
import ml_dtypes


def mxq(x, axis, fmt="e4m3"):
    dtype, down = {"e4m3": (ml_dtypes.float8_e4m3fn, 7), "e5m2": (ml_dtypes.float8_e5m2, 14)}[fmt]
    v = np.moveaxis(np.asarray(x, np.float32).astype(ml_dtypes.bfloat16).astype(np.float64), axis, -1)
    blocks = v.reshape(v.shape[:-1] + (-1, 32))
    amax = np.abs(blocks).max(-1, keepdims=True)
    byte = np.maximum(np.where(amax > 0, np.frexp(amax)[1] - 1 + 127, 0) - down, 1)
    scale = np.exp2(byte - 127.0)
    codes = (blocks / scale).astype(np.float32).astype(dtype).astype(np.float64)
    return np.moveaxis((codes * scale).reshape(v.shape), -1, axis)


WIDE = False


def mx_kscale(k):
    if not WIDE:
        return np.ones(k)
    levels = np.array([10, -10, 5, -5, 0])
    if k % 512:
        return np.exp2(np.random.permutation(np.resize(levels, k // 32))).repeat(32)
    a = np.empty((k // 512, 16))
    for p in range(k // 512):
        a[p, :8] = np.random.permutation(np.resize(levels, 8))
        for g in range(8):
            far = levels[np.abs(levels - a[p, g]) >= 10]
            a[p, g + 8] = far[np.random.randint(len(far))]
    return np.exp2(a.ravel()).repeat(32)


def f64(x):
    return np.asarray(x).astype(np.float64)


def striped(idx):
    return np.tile(idx.reshape(-1, 16).T, (8, 1)).astype(np.uint16)


def unstriped(offs):
    return offs[:16].T.reshape(-1).astype(np.int64)


E2M1 = np.array([0.0, 0.5, 1.0, 1.5, 2.0, 3.0, 4.0, 6.0, -0.0, -0.5, -1.0, -1.5, -2.0, -3.0, -4.0, -6.0])


def pack_weight(w, fmt):
    k, n = w.shape
    w = f64(np.asarray(w, np.float32).astype(ml_dtypes.bfloat16)).reshape(k // 32, 32, n)
    amax = np.abs(w).max(1)
    if fmt == "e4m3":
        byte = np.frexp(amax)[1] - 1 + 127 - 7
    else:
        mant, ex = np.frexp(amax / 6.0)
        byte = np.where(mant > 0.5, ex, ex - 1) + 127
    byte = np.clip(np.where(amax > 0, byte, 1), 1, 254)
    scaled = (w * np.exp2(127.0 - byte)[:, None, :]).reshape(k, n).astype(np.float32)
    by_word = np.ascontiguousarray(scaled.reshape(k // 512, 128, 4, n).transpose(0, 1, 3, 2))
    if fmt == "e4m3":
        words = by_word.astype(ml_dtypes.float8_e4m3fn).view(np.uint8)
    else:
        c = by_word.astype(ml_dtypes.float4_e2m1fn).view(np.uint8) & 0xF
        words = (c[..., 0::2] | (c[..., 1::2] << 4)).reshape(k // 512, 128, 2 * n)
    return np.ascontiguousarray(words), np.ascontiguousarray(byte.astype(np.uint8).reshape(k // 512, 16, n))


def unpack_weight(words, scales, fmt):
    g, _, n = scales.shape
    words = np.ascontiguousarray(words).reshape(g, 128, n, -1)
    if fmt == "e4m3":
        vals = words.view(ml_dtypes.float8_e4m3fn).astype(np.float64)
    else:
        nib = np.empty((g, 128, n, 4), np.uint8)
        nib[..., 0::2] = words & 0xF
        nib[..., 1::2] = words >> 4
        vals = E2M1[nib]
    vals = vals * np.repeat(np.exp2(scales.astype(np.float64) - 127.0), 8, axis=1)[..., None]
    return vals.transpose(0, 1, 3, 2).reshape(g * 512, n)


def gelu(v):
    return 0.5 * v * (1.0 + np.tanh(np.sqrt(2.0 / np.pi) * (v + 0.044715 * v**3)))


K, D, T, S, T2, S2, N = 1024, 512, 4096, 1536, 1024, 512, 512


def setup_inputs():
    n = np.random.standard_normal
    s = mx_kscale(K)[:, None]
    u = mx_kscale(S)
    tab_words, tab_scales = pack_weight(n((K, T)) * s, "e4m3")
    tab2_words, tab2_scales = pack_weight(0.7 * n((K, T2)) / np.sqrt(D) / s, "e4m3")
    w4_words, w4_scales = pack_weight(n((S, N)) / np.sqrt(S) / u[:, None], "e2m1")
    return {
        "tab_words": tab_words, "tab_scales": tab_scales,
        "tab2_words": tab2_words, "tab2_scales": tab2_scales,
        "offs": striped(np.random.permutation(T)[:S]),
        "offs2": striped(np.random.permutation(T2)[:S2]),
        "lam": (0.4 * np.exp(0.2 * n(S))).astype(np.float32),
        "tw": (np.exp(0.3 * n(S)) * u).astype(np.float32),
        "w4_words": w4_words, "w4_scales": w4_scales,
        "wu": (0.6 * n((S, N)) / np.sqrt(S) / u[:, None]).astype(np.float32),
    }


def reference(tab_words, tab_scales, tab2_words, tab2_scales, offs, offs2, lam, tw, w4_words, w4_scales, wu):
    v = unpack_weight(tab_words, tab_scales, "e4m3")[:, unstriped(offs)]
    v2 = unpack_weight(tab2_words, tab2_scales, "e4m3")[:, unstriped(offs2)]
    w4 = unpack_weight(w4_words, w4_scales, "e2m1")
    wuq = mxq(f64(wu), 0, "e4m3")
    a1 = v[:D].T @ v2[:D]
    a2 = v[D:].T @ v2[D:]
    z = (np.exp(a1) - f64(lam)[:, None] * np.exp(a2)) * f64(tw)[:, None]
    zq = mxq(z, 0, "e4m3")
    return w4.T @ zq + wuq.T @ zq

@@ -1,0 +1,267 @@
+from contextlib import ExitStack
+
+import concourse.mybir as mybir
+
+K, D, T, S, T2, S2, N = 1024, 512, 4096, 1536, 1024, 512, 512
+FLOPS = 2 * K * S * S2 + 2 * 2 * S * N * S2
+
+F32 = mybir.dt.float32
+BF16 = mybir.dt.bfloat16
+I32 = mybir.dt.int32
+U32 = mybir.dt.uint32
+U16 = mybir.dt.uint16
+U8 = mybir.dt.uint8
+FP8X4 = mybir.dt.float8_e4m3fn_x4
+FP4X4 = mybir.dt.float4_e2m1fn_x4
+ALU = mybir.AluOpType
+ACT = mybir.ActivationFunctionType
+
+P = 128
+PACK = 4
+PASS = P * PACK
+HALVES = K // D
+PASSES = S // PASS
+BLOCKS = N // P
+QUADS = 4
+KEY_ROW = (0, 4)
+QUERY_ROW = (8, 12)
+LN_EDGE = 2.0 ** 64
+
+
+def woven(ap):
+    return ap.rearrange("p (c i t) -> p c t i", i=4, t=PACK)
+
+
+def planes(ap):
+    return ap.rearrange("p t (c i) -> p c t i", i=4)
+
+
+def tile_list_differential_exp_mix_kernel(
+    tc, tab_words, tab_scales, tab2_words, tab2_scales, offs, offs2, lam, tw, w4_words, w4_scales, wu, out
+):
+    nc = tc.nc
+    with ExitStack() as ctx:
+        keep = ctx.enter_context(tc.tile_pool(name="keep", bufs=1))
+        score_banks = ctx.enter_context(tc.psum_pool(name="score_banks", bufs=4))
+        out_banks = ctx.enter_context(tc.psum_pool(name="out_banks", bufs=1))
+
+        def held(name, shape, dtype):
+            return keep.tile(shape, dtype, name=name, align_bytes=64)
+
+        key_list = keep.tile([P, S // 16], U16, name="key_list")
+        query_list = keep.tile([P, S2 // 16], U16, name="query_list")
+        key_table = [held("key_table%d" % h, [P, T], I32) for h in range(HALVES)]
+        query_table = [held("query_table%d" % h, [P, T2], I32) for h in range(HALVES)]
+        key_scale_table = held("key_scale_table", [P, T], U8)
+        query_scale_table = held("query_scale_table", [P, T2], U8)
+        w4_codes = held("w4_codes", [P, PASSES, 2 * N], U8)
+        w4_scale = held("w4_scale", [P, PASSES, N], U8)
+        wu_rows = [held("wu_rows%d" % a, [P, PACK, N], F32) for a in range(PASSES)]
+        factors = held("factors", [P, 2, 16], F32)
+
+        def words(table, h):
+            return table[h].rearrange("p n t -> p (n t)").bitcast(I32)
+
+        nc.vector.memset(query_scale_table[:].bitcast(I32), 0)
+        nc.vector.memset(key_scale_table[:].bitcast(I32), 0)
+        nc.vector.memset(w4_scale[:].rearrange("p a n -> p (a n)").bitcast(I32), 0)
+
+        nc.sync.dma_start(query_list[:], offs2)
+        nc.sync.dma_start(query_table[0][:], words(tab2_words, 0))
+        nc.sync.dma_start(key_list[:], offs)
+        for q in range(QUADS):
+            nc.sync.dma_start(
+                query_scale_table[32 * q + QUERY_ROW[0] : 32 * q + QUERY_ROW[0] + 8, :].bitcast(I32),
+                tab2_scales[:, 4 * q : 4 * q + 4, :].bitcast(I32),
+            )
+        for q in range(QUADS):
+            nc.scalar.dma_start(
+                key_scale_table[32 * q : 32 * q + 8, :].bitcast(I32),
+                tab_scales[:, 4 * q : 4 * q + 4, :].bitcast(I32),
+            )
+        for s, vec in enumerate((tw, lam)):
+            nc.scalar.dma_start(
+                factors[:, s, : PASSES * PACK].rearrange("p (a t) -> p a t", t=PACK),
+                vec.rearrange("(a p t) -> p a t", p=P, t=PACK),
+            )
+        nc.sync.dma_start(query_table[1][:], words(tab2_words, 1))
+        nc.sync.dma_start(key_table[0][:], words(tab_words, 0))
+        nc.sync.dma_start(key_table[1][:], words(tab_words, 1))
+
+        def load_wu(a):
+            nc.sync.dma_start(wu_rows[a][:], wu[a * PASS : (a + 1) * PASS, :].rearrange("(p t) n -> p t n", t=PACK))
+
+        load_wu(0)
+        nc.sync.dma_start(w4_codes[:].bitcast(I32), w4_words.rearrange("a p n -> p a n").bitcast(I32))
+        for q in range(QUADS):
+            nc.sync.dma_start(
+                w4_scale[32 * q : 32 * q + 4, :, :].bitcast(I32),
+                w4_scales[:, 4 * q : 4 * q + 4, :].rearrange("a r n -> r a n").bitcast(I32),
+            )
+        load_wu(1)
+        load_wu(2)
+
+        query_codes = [held("query_codes%d" % h, [P, S2], U32) for h in range(HALVES)]
+        query_scale = held("query_scale", [P, S2], U8)
+        nc.vector.tensor_copy(query_codes[0][:], query_table[0][:].bitcast(U32).indirect(query_list[:]))
+        nc.vector.tensor_copy(query_scale[:], query_scale_table[:].indirect(query_list[:]))
+        nc.vector.tensor_copy(query_codes[1][:], query_table[1][:].bitcast(U32).indirect(query_list[:]))
+
+        key_scale_listed = {}
+        key_scale = [held("key_scale%d" % a, [P, PACK, P], U8) for a in range(PASSES)]
+        key_codes = {}
+
+        def entries(a):
+            return key_list[:, a * PASS // 16 : (a + 1) * PASS // 16]
+
+        def gather_key_scales(a):
+            slot = "key_codes0_0" if a == PASSES - 1 else "key_scale_listed%d" % a
+            key_scale_listed[a] = keep.tile([P, PASS], U8, name="key_scale_listed%d" % a, tag=slot, align_bytes=64)
+            nc.vector.tensor_copy(key_scale_listed[a][:], key_scale_table[:].indirect(entries(a)))
+
+        def order_key_scales(a):
+            nc.vector.tensor_copy(
+                key_scale[a][:].rearrange("p t m -> p m t"), key_scale_listed[a][:].rearrange("p (m t) -> p m t", t=PACK)
+            )
+
+        def gather_keys(h, a):
+            key_codes[h, a] = held("key_codes%d_%d" % (h, a), [P, PACK, P], U32)
+            nc.vector.tensor_copy(
+                key_codes[h, a][:].rearrange("p t m -> p m t"), key_table[h][:].bitcast(U32).indirect(entries(a))
+            )
+
+        parts = held("parts", [P, 2, 3, PASSES * PACK], F32)
+        logs = held("logs", [P, 2, 3, PASSES * PACK], F32)
+        bias = held("bias", [P, HALVES, PASSES * PACK], F32)
+
+        def split_factors():
+            given = factors[:, :, : PASSES * PACK]
+            nc.vector.tensor_scalar(parts[:, :, 0, :], given, 1.0 / LN_EDGE, LN_EDGE, ALU.max, ALU.min)
+            nc.vector.tensor_scalar(parts[:, :, 1, :], given, 1.0 / LN_EDGE, 1.0, ALU.mult, ALU.max)
+            nc.vector.tensor_scalar(parts[:, :, 2, :], given, LN_EDGE, 1.0, ALU.mult, ALU.min)
+            nc.scalar.activation(
+                logs[:].rearrange("p s k c -> p (s k c)"), parts[:].rearrange("p s k c -> p (s k c)"), ACT.Ln
+            )
+
+        def sum_logs():
+            terms = logs[:].rearrange("p s k c -> p c (s k)")
+            nc.vector.tensor_reduce(bias[:, 0, :], terms[:, :, 0:3], mybir.AxisListType.X, ALU.add)
+            nc.vector.tensor_reduce(bias[:, 1, :], terms, mybir.AxisListType.X, ALU.add)
+
+        terms_exp = [[held("exp%d_%d" % (h, a), [P, PACK, S2], F32) for a in range(PASSES)] for h in range(HALVES)]
+
+        def scores(h, a):
+            for t in range(PACK):
+                bank = score_banks.tile([P, S2], F32, name="bank")
+                nc.tensor.matmul_mx(
+                    out=bank[:],
+                    lhsT=key_codes[h, a][:, t, :].bitcast(FP8X4),
+                    lhsT_scale=key_scale[a][KEY_ROW[h] :, t, :],
+                    rhs=query_codes[h][:].bitcast(FP8X4),
+                    rhs_scale=query_scale[QUERY_ROW[h] :, :],
+                    start=True,
+                    stop=True,
+                )
+                c = a * PACK + t
+                nc.scalar.activation(terms_exp[h][a][:, t, :], bank[:], ACT.Exp, bias=bias[:, h, c : c + 1])
+
+        z_woven = [held("z_woven%d" % a, [P, S2 * PACK], BF16) for a in range(PASSES)]
+        z_codes = [held("z_codes%d" % a, [P, S2], U32) for a in range(PASSES)]
+        z_scale = [held("z_scale%d" % a, [P, S2], U8) for a in range(PASSES)]
+        wu_woven = [held("wu_woven%d" % a, [P, N * PACK], BF16) for a in range(PASSES)]
+        wu_codes = [held("wu_codes%d" % a, [P, N], U32) for a in range(PASSES)]
+        wu_scale = [held("wu_scale%d" % a, [P, N], U8) for a in range(PASSES)]
+
+        def difference(a):
+            nc.vector.tensor_tensor(
+                woven(z_woven[a][:]), planes(terms_exp[0][a][:]), planes(terms_exp[1][a][:]), ALU.subtract
+            )
+
+        def quantise_z(a):
+            nc.vector.quantize_mx(out=z_codes[a][:].bitcast(FP8X4), scales=z_scale[a][:], in_=z_woven[a][:])
+
+        def weave_wu(a, copy, cols):
+            copy(woven(wu_woven[a][:, PACK * cols.start : PACK * cols.stop]), planes(wu_rows[a][:, :, cols]))
+
+        def quantise_wu(a, cols):
+            nc.vector.quantize_mx(
+                out=wu_codes[a][:, cols].bitcast(FP8X4),
+                scales=wu_scale[a][:, cols],
+                in_=wu_woven[a][:, PACK * cols.start : PACK * cols.stop],
+            )
+
+        sums = [out_banks.tile([P, S2], F32, name="sum%d" % b) for b in range(BLOCKS)]
+
+        def mix_w4(a, b):
+            nc.tensor.matmul_mx(
+                out=sums[b][:],
+                lhsT=w4_codes[:, a, 2 * P * b : 2 * P * (b + 1)].bitcast(FP4X4),
+                lhsT_scale=w4_scale[:, a, P * b : P * (b + 1)],
+                rhs=z_codes[a][:].bitcast(FP8X4),
+                rhs_scale=z_scale[a][:],
+                start=(a == 0),
+                stop=False,
+            )
+
+        def mix_wu(a, b):
+            nc.tensor.matmul_mx(
+                out=sums[b][:],
+                lhsT=wu_codes[a][:, P * b : P * (b + 1)].bitcast(FP8X4),
+                lhsT_scale=wu_scale[a][:, P * b : P * (b + 1)],
+                rhs=z_codes[a][:].bitcast(FP8X4),
+                rhs_scale=z_scale[a][:],
+                start=False,
+                stop=(a == PASSES - 1),
+            )
+
+        whole = slice(0, N)
+        block = [slice(P * b, P * (b + 1)) for b in range(BLOCKS)]
+        gather_key_scales(0)
+        split_factors()
+        order_key_scales(0)
+        gather_key_scales(1)
+        sum_logs()
+        gather_keys(0, 0)
+        order_key_scales(1)
+        scores(0, 0)
+        gather_keys(0, 1)
+        scores(0, 1)
+        gather_keys(0, 2)
+        gather_key_scales(2)
+        gather_keys(1, 0)
+        order_key_scales(2)
+        scores(0, 2)
+        scores(1, 0)
+        gather_keys(1, 1)
+        scores(1, 1)
+        gather_keys(1, 2)
+        scores(1, 2)
+        weave_wu(0, nc.vector.tensor_copy, whole)
+        difference(0)
+        quantise_wu(0, whole)
+        quantise_z(0)
+        for b in range(BLOCKS):
+            mix_w4(0, b)
+            mix_wu(0, b)
+        difference(1)
+        weave_wu(1, nc.scalar.copy, whole)
+        quantise_z(1)
+        for b in range(BLOCKS):
+            mix_w4(1, b)
+        difference(2)
+        quantise_wu(1, whole)
+        for b in range(BLOCKS):
+            mix_wu(1, b)
+        quantise_z(2)
+        for b in range(BLOCKS):
+            weave_wu(2, nc.scalar.copy, block[b])
+            quantise_wu(2, block[b])
+        results = [held("result%d" % b, [P, S2], F32) for b in range(BLOCKS)]
+        for b in range(BLOCKS):
+            mix_w4(2, b)
+            mix_wu(2, b)
+            if b % 2 == 0:
+                nc.scalar.copy(results[b][:], sums[b][:])
+            else:
+                nc.vector.tensor_copy(results[b][:], sums[b][:])
+            nc.sync.dma_start(out[P * b : P * (b + 1), :], results[b][:])

@@ -75,12 +75,12 @@ def tile_list_differential_exp_mix_kernel(
                 tab2_scales[:, 4 * q : 4 * q + 4, :].bitcast(I32),
             )
         for q in range(QUADS):
-            nc.scalar.dma_start(
+            nc.gpsimd.dma_start(
                 key_scale_table[32 * q : 32 * q + 8, :].bitcast(I32),
                 tab_scales[:, 4 * q : 4 * q + 4, :].bitcast(I32),
             )
         for s, vec in enumerate((tw, lam)):
-            nc.scalar.dma_start(
+            nc.gpsimd.dma_start(
                 factors[:, s, : PASSES * PACK].rearrange("p (a t) -> p a t", t=PACK),
                 vec.rearrange("(a p t) -> p a t", p=P, t=PACK),
             )
@@ -121,7 +121,7 @@ def tile_list_differential_exp_mix_kernel(
 
         def order_key_scales(a):
             nc.vector.tensor_copy(
-                key_scale[a][:].rearrange("p t m -> p m t"), key_scale_listed[a][:].rearrange("p (m t) -> p m t", t=PACK)
+                key_scale[a][:], key_scale_listed[a][:].rearrange("p (m t) -> p t m", t=PACK)
             )
 
         def gather_keys(h, a):

@@ -42,7 +42,7 @@ def tile_list_differential_exp_mix_kernel(
     nc = tc.nc
     with ExitStack() as ctx:
         keep = ctx.enter_context(tc.tile_pool(name="keep", bufs=1))
-        score_banks = ctx.enter_context(tc.psum_pool(name="score_banks", bufs=4))
+        score_banks = ctx.enter_context(tc.psum_pool(name="score_banks", bufs=1))
         out_banks = ctx.enter_context(tc.psum_pool(name="out_banks", bufs=1))
 
         def held(name, shape, dtype):
@@ -62,30 +62,30 @@ def tile_list_differential_exp_mix_kernel(
         def words(table, h):
             return table[h].rearrange("p n t -> p (n t)").bitcast(I32)
 
-        nc.vector.memset(query_scale_table[:].bitcast(I32), 0)
+        nc.gpsimd.memset(query_scale_table[:].bitcast(I32), 0)
         nc.vector.memset(key_scale_table[:].bitcast(I32), 0)
         nc.vector.memset(w4_scale[:].rearrange("p a n -> p (a n)").bitcast(I32), 0)
 
         nc.sync.dma_start(query_list[:], offs2)
-        nc.sync.dma_start(query_table[0][:], words(tab2_words, 0))
-        nc.sync.dma_start(key_list[:], offs)
         for q in range(QUADS):
             nc.sync.dma_start(
                 query_scale_table[32 * q + QUERY_ROW[0] : 32 * q + QUERY_ROW[0] + 8, :].bitcast(I32),
                 tab2_scales[:, 4 * q : 4 * q + 4, :].bitcast(I32),
             )
-        for q in range(QUADS):
-            nc.gpsimd.dma_start(
-                key_scale_table[32 * q : 32 * q + 8, :].bitcast(I32),
-                tab_scales[:, 4 * q : 4 * q + 4, :].bitcast(I32),
-            )
         for s, vec in enumerate((tw, lam)):
-            nc.gpsimd.dma_start(
+            nc.sync.dma_start(
                 factors[:, s, : PASSES * PACK].rearrange("p (a t) -> p a t", t=PACK),
                 vec.rearrange("(a p t) -> p a t", p=P, t=PACK),
             )
-        nc.sync.dma_start(query_table[1][:], words(tab2_words, 1))
+        nc.sync.dma_start(query_table[0][:], words(tab2_words, 0))
+        nc.sync.dma_start(key_list[:], offs)
+        for q in range(QUADS):
+            nc.sync.dma_start(
+                key_scale_table[32 * q : 32 * q + 8, :].bitcast(I32),
+                tab_scales[:, 4 * q : 4 * q + 4, :].bitcast(I32),
+            )
         nc.sync.dma_start(key_table[0][:], words(tab_words, 0))
+        nc.sync.dma_start(query_table[1][:], words(tab2_words, 1))
         nc.sync.dma_start(key_table[1][:], words(tab_words, 1))
 
         def load_wu(a):
@@ -103,26 +103,22 @@ def tile_list_differential_exp_mix_kernel(
 
         query_codes = [held("query_codes%d" % h, [P, S2], U32) for h in range(HALVES)]
         query_scale = held("query_scale", [P, S2], U8)
-        nc.vector.tensor_copy(query_codes[0][:], query_table[0][:].bitcast(U32).indirect(query_list[:]))
-        nc.vector.tensor_copy(query_scale[:], query_scale_table[:].indirect(query_list[:]))
-        nc.vector.tensor_copy(query_codes[1][:], query_table[1][:].bitcast(U32).indirect(query_list[:]))
 
-        key_scale_listed = {}
-        key_scale = [held("key_scale%d" % a, [P, PACK, P], U8) for a in range(PASSES)]
+        def gather_queries(h):
+            nc.vector.tensor_copy(query_codes[h][:], query_table[h][:].bitcast(U32).indirect(query_list[:]))
+
+        key_scale_listed = held("key_scale_listed", [P, S], U8)
+        key_scale = held("key_scale", [P, PACK, S // PACK], U8)
         key_codes = {}
 
         def entries(a):
             return key_list[:, a * PASS // 16 : (a + 1) * PASS // 16]
 
-        def gather_key_scales(a):
-            slot = "key_codes0_0" if a == PASSES - 1 else "key_scale_listed%d" % a
-            key_scale_listed[a] = keep.tile([P, PASS], U8, name="key_scale_listed%d" % a, tag=slot, align_bytes=64)
-            nc.vector.tensor_copy(key_scale_listed[a][:], key_scale_table[:].indirect(entries(a)))
+        def gather_key_scales():
+            nc.vector.tensor_copy(key_scale_listed[:], key_scale_table[:].indirect(key_list[:]))
 
-        def order_key_scales(a):
-            nc.vector.tensor_copy(
-                key_scale[a][:], key_scale_listed[a][:].rearrange("p (m t) -> p t m", t=PACK)
-            )
+        def order_key_scales():
+            nc.vector.tensor_copy(key_scale[:], key_scale_listed[:].rearrange("p (m t) -> p t m", t=PACK))
 
         def gather_keys(h, a):
             key_codes[h, a] = held("key_codes%d_%d" % (h, a), [P, PACK, P], U32)
@@ -130,33 +126,35 @@ def tile_list_differential_exp_mix_kernel(
                 key_codes[h, a][:].rearrange("p t m -> p m t"), key_table[h][:].bitcast(U32).indirect(entries(a))
             )
 
-        parts = held("parts", [P, 2, 3, PASSES * PACK], F32)
-        logs = held("logs", [P, 2, 3, PASSES * PACK], F32)
-        bias = held("bias", [P, HALVES, PASSES * PACK], F32)
+        ROWS = PASSES * PACK
+        parts = held("parts", [P, ROWS, 2, 3], F32)
+        logs = held("logs", [P, ROWS, 2, 3], F32)
+        bias = held("bias", [P, HALVES, ROWS], F32)
 
         def split_factors():
-            given = factors[:, :, : PASSES * PACK]
-            nc.vector.tensor_scalar(parts[:, :, 0, :], given, 1.0 / LN_EDGE, LN_EDGE, ALU.max, ALU.min)
-            nc.vector.tensor_scalar(parts[:, :, 1, :], given, 1.0 / LN_EDGE, 1.0, ALU.mult, ALU.max)
-            nc.vector.tensor_scalar(parts[:, :, 2, :], given, LN_EDGE, 1.0, ALU.mult, ALU.min)
-            nc.scalar.activation(
-                logs[:].rearrange("p s k c -> p (s k c)"), parts[:].rearrange("p s k c -> p (s k c)"), ACT.Ln
-            )
+            given = factors[:, :, :ROWS].rearrange("p s c -> p c s")
+            nc.vector.tensor_scalar(parts[:, :, :, 0], given, 1.0 / LN_EDGE, LN_EDGE, ALU.max, ALU.min)
+            nc.vector.tensor_scalar(parts[:, :, :, 1], given, 1.0 / LN_EDGE, 1.0, ALU.mult, ALU.max)
+            nc.vector.tensor_scalar(parts[:, :, :, 2], given, LN_EDGE, 1.0, ALU.mult, ALU.min)
 
         def sum_logs():
-            terms = logs[:].rearrange("p s k c -> p c (s k)")
-            nc.vector.tensor_reduce(bias[:, 0, :], terms[:, :, 0:3], mybir.AxisListType.X, ALU.add)
-            nc.vector.tensor_reduce(bias[:, 1, :], terms, mybir.AxisListType.X, ALU.add)
+            for h in range(HALVES):
+                for c in range(ROWS):
+                    nc.scalar.activation(
+                        logs[:, c, : h + 1, :], parts[:, c, : h + 1, :], ACT.Ln, accum_out=bias[:, h, c : c + 1]
+                    )
 
         terms_exp = [[held("exp%d_%d" % (h, a), [P, PACK, S2], F32) for a in range(PASSES)] for h in range(HALVES)]
 
+        banks = [score_banks.tile([P, S2], F32, name="bank%d" % t) for t in range(PACK)]
+
         def scores(h, a):
             for t in range(PACK):
-                bank = score_banks.tile([P, S2], F32, name="bank")
+                bank = banks[t]
                 nc.tensor.matmul_mx(
                     out=bank[:],
                     lhsT=key_codes[h, a][:, t, :].bitcast(FP8X4),
-                    lhsT_scale=key_scale[a][KEY_ROW[h] :, t, :],
+                    lhsT_scale=key_scale[KEY_ROW[h] :, t, P * a : P * (a + 1)],
                     rhs=query_codes[h][:].bitcast(FP8X4),
                     rhs_scale=query_scale[QUERY_ROW[h] :, :],
                     start=True,
@@ -172,9 +170,12 @@ def tile_list_differential_exp_mix_kernel(
         wu_codes = [held("wu_codes%d" % a, [P, N], U32) for a in range(PASSES)]
         wu_scale = [held("wu_scale%d" % a, [P, N], U8) for a in range(PASSES)]
 
-        def difference(a):
+        def difference(a, cols):
             nc.vector.tensor_tensor(
-                woven(z_woven[a][:]), planes(terms_exp[0][a][:]), planes(terms_exp[1][a][:]), ALU.subtract
+                woven(z_woven[a][:, PACK * cols.start : PACK * cols.stop]),
+                planes(terms_exp[0][a][:, :, cols]),
+                planes(terms_exp[1][a][:, :, cols]),
+                ALU.subtract,
             )
 
         def quantise_z(a):
@@ -216,42 +217,37 @@ def tile_list_differential_exp_mix_kernel(
 
         whole = slice(0, N)
         block = [slice(P * b, P * (b + 1)) for b in range(BLOCKS)]
-        gather_key_scales(0)
+        nc.vector.tensor_copy(query_scale[:], query_scale_table[:].indirect(query_list[:]))
         split_factors()
-        order_key_scales(0)
-        gather_key_scales(1)
         sum_logs()
-        gather_keys(0, 0)
-        order_key_scales(1)
-        scores(0, 0)
-        gather_keys(0, 1)
-        scores(0, 1)
-        gather_keys(0, 2)
-        gather_key_scales(2)
-        gather_keys(1, 0)
-        order_key_scales(2)
-        scores(0, 2)
-        scores(1, 0)
-        gather_keys(1, 1)
-        scores(1, 1)
-        gather_keys(1, 2)
-        scores(1, 2)
+        gather_queries(0)
+        gather_key_scales()
+        order_key_scales()
+        for a in range(PASSES):
+            gather_keys(0, a)
+        gather_queries(1)
+        for a in range(PASSES):
+            gather_keys(1, a)
+        for h, a in ((0, 0), (0, 1), (1, 0), (1, 1), (0, 2), (1, 2)):
+            scores(h, a)
+        half = [slice(0, N // 2), slice(N // 2, N)]
         weave_wu(0, nc.vector.tensor_copy, whole)
-        difference(0)
+        difference(0, whole)
         quantise_wu(0, whole)
         quantise_z(0)
         for b in range(BLOCKS):
             mix_w4(0, b)
             mix_wu(0, b)
-        difference(1)
-        weave_wu(1, nc.scalar.copy, whole)
+        difference(1, whole)
         quantise_z(1)
         for b in range(BLOCKS):
             mix_w4(1, b)
-        difference(2)
-        quantise_wu(1, whole)
-        for b in range(BLOCKS):
-            mix_wu(1, b)
+        for u in range(2):
+            weave_wu(1, nc.scalar.copy, half[u])
+            difference(2, half[u])
+            quantise_wu(1, half[u])
+            mix_wu(1, 2 * u)
+            mix_wu(1, 2 * u + 1)
         quantise_z(2)
         for b in range(BLOCKS):
             weave_wu(2, nc.scalar.copy, block[b])

@@ -62,27 +62,27 @@ def tile_list_differential_exp_mix_kernel(
         def words(table, h):
             return table[h].rearrange("p n t -> p (n t)").bitcast(I32)
 
-        nc.gpsimd.memset(query_scale_table[:].bitcast(I32), 0)
         nc.vector.memset(key_scale_table[:].bitcast(I32), 0)
-        nc.vector.memset(w4_scale[:].rearrange("p a n -> p (a n)").bitcast(I32), 0)
+        nc.vector.memset(query_scale_table[:].bitcast(I32), 0)
+        nc.gpsimd.memset(w4_scale[:].rearrange("p a n -> p (a n)").bitcast(I32), 0)
 
         nc.sync.dma_start(query_list[:], offs2)
-        for q in range(QUADS):
-            nc.sync.dma_start(
-                query_scale_table[32 * q + QUERY_ROW[0] : 32 * q + QUERY_ROW[0] + 8, :].bitcast(I32),
-                tab2_scales[:, 4 * q : 4 * q + 4, :].bitcast(I32),
-            )
+        nc.sync.dma_start(key_list[:], offs)
+        nc.sync.dma_start(query_table[0][:], words(tab2_words, 0))
         for s, vec in enumerate((tw, lam)):
             nc.sync.dma_start(
                 factors[:, s, : PASSES * PACK].rearrange("p (a t) -> p a t", t=PACK),
                 vec.rearrange("(a p t) -> p a t", p=P, t=PACK),
             )
-        nc.sync.dma_start(query_table[0][:], words(tab2_words, 0))
-        nc.sync.dma_start(key_list[:], offs)
         for q in range(QUADS):
             nc.sync.dma_start(
                 key_scale_table[32 * q : 32 * q + 8, :].bitcast(I32),
                 tab_scales[:, 4 * q : 4 * q + 4, :].bitcast(I32),
+            )
+        for q in range(QUADS):
+            nc.scalar.dma_start(
+                query_scale_table[32 * q + QUERY_ROW[0] : 32 * q + QUERY_ROW[0] + 8, :].bitcast(I32),
+                tab2_scales[:, 4 * q : 4 * q + 4, :].bitcast(I32),
             )
         nc.sync.dma_start(key_table[0][:], words(tab_words, 0))
         nc.sync.dma_start(query_table[1][:], words(tab2_words, 1))
@@ -217,10 +217,10 @@ def tile_list_differential_exp_mix_kernel(
 
         whole = slice(0, N)
         block = [slice(P * b, P * (b + 1)) for b in range(BLOCKS)]
-        nc.vector.tensor_copy(query_scale[:], query_scale_table[:].indirect(query_list[:]))
+        gather_queries(0)
         split_factors()
         sum_logs()
-        gather_queries(0)
+        nc.vector.tensor_copy(query_scale[:], query_scale_table[:].indirect(query_list[:]))
         gather_key_scales()
         order_key_scales()
         for a in range(PASSES):

from contextlib import ExitStack

import concourse.mybir as mybir

K, D, T, S, T2, S2, N = 1024, 512, 4096, 1536, 1024, 512, 512
FLOPS = 2 * K * S * S2 + 2 * 2 * S * N * S2

F32 = mybir.dt.float32
BF16 = mybir.dt.bfloat16
I32 = mybir.dt.int32
U32 = mybir.dt.uint32
U16 = mybir.dt.uint16
U8 = mybir.dt.uint8
FP8X4 = mybir.dt.float8_e4m3fn_x4
FP4X4 = mybir.dt.float4_e2m1fn_x4
ALU = mybir.AluOpType
ACT = mybir.ActivationFunctionType

P = 128
PACK = 4
PASS = P * PACK
HALVES = K // D
PASSES = S // PASS
BLOCKS = N // P
QUADS = 4
KEY_ROW = (0, 4)
QUERY_ROW = (8, 12)
LN_EDGE = 2.0 ** 64


def woven(ap):
    return ap.rearrange("p (c i t) -> p c t i", i=4, t=PACK)


def planes(ap):
    return ap.rearrange("p t (c i) -> p c t i", i=4)


def tile_list_differential_exp_mix_kernel(
    tc, tab_words, tab_scales, tab2_words, tab2_scales, offs, offs2, lam, tw, w4_words, w4_scales, wu, out
):
    nc = tc.nc
    with ExitStack() as ctx:
        keep = ctx.enter_context(tc.tile_pool(name="keep", bufs=1))
        score_banks = ctx.enter_context(tc.psum_pool(name="score_banks", bufs=1))
        out_banks = ctx.enter_context(tc.psum_pool(name="out_banks", bufs=1))

        def held(name, shape, dtype):
            return keep.tile(shape, dtype, name=name, align_bytes=64)

        key_list = keep.tile([P, S // 16], U16, name="key_list")
        query_list = keep.tile([P, S2 // 16], U16, name="query_list")
        key_table = [held("key_table%d" % h, [P, T], I32) for h in range(HALVES)]
        query_table = [held("query_table%d" % h, [P, T2], I32) for h in range(HALVES)]
        key_scale_table = held("key_scale_table", [P, T], U8)
        query_scale_table = held("query_scale_table", [P, T2], U8)
        w4_codes = held("w4_codes", [P, PASSES, 2 * N], U8)
        w4_scale = held("w4_scale", [P, PASSES, N], U8)
        wu_rows = [held("wu_rows%d" % a, [P, PACK, N], F32) for a in range(PASSES)]
        factors = held("factors", [P, 2, 16], F32)

        def words(table, h):
            return table[h].rearrange("p n t -> p (n t)").bitcast(I32)

        nc.vector.memset(key_scale_table[:].bitcast(I32), 0)
        nc.vector.memset(query_scale_table[:].bitcast(I32), 0)
        nc.gpsimd.memset(w4_scale[:].rearrange("p a n -> p (a n)").bitcast(I32), 0)

        nc.sync.dma_start(query_list[:], offs2)
        nc.sync.dma_start(key_list[:], offs)
        nc.sync.dma_start(query_table[0][:], words(tab2_words, 0))
        for s, vec in enumerate((tw, lam)):
            nc.sync.dma_start(
                factors[:, s, : PASSES * PACK].rearrange("p (a t) -> p a t", t=PACK),
                vec.rearrange("(a p t) -> p a t", p=P, t=PACK),
            )
        for q in range(QUADS):
            nc.sync.dma_start(
                key_scale_table[32 * q : 32 * q + 8, :].bitcast(I32),
                tab_scales[:, 4 * q : 4 * q + 4, :].bitcast(I32),
            )
        for q in range(QUADS):
            nc.scalar.dma_start(
                query_scale_table[32 * q + QUERY_ROW[0] : 32 * q + QUERY_ROW[0] + 8, :].bitcast(I32),
                tab2_scales[:, 4 * q : 4 * q + 4, :].bitcast(I32),
            )
        nc.sync.dma_start(key_table[0][:], words(tab_words, 0))
        nc.sync.dma_start(query_table[1][:], words(tab2_words, 1))
        nc.sync.dma_start(key_table[1][:], words(tab_words, 1))

        def load_wu(a):
            nc.sync.dma_start(wu_rows[a][:], wu[a * PASS : (a + 1) * PASS, :].rearrange("(p t) n -> p t n", t=PACK))

        load_wu(0)
        nc.sync.dma_start(w4_codes[:].bitcast(I32), w4_words.rearrange("a p n -> p a n").bitcast(I32))
        for q in range(QUADS):
            nc.sync.dma_start(
                w4_scale[32 * q : 32 * q + 4, :, :].bitcast(I32),
                w4_scales[:, 4 * q : 4 * q + 4, :].rearrange("a r n -> r a n").bitcast(I32),
            )
        load_wu(1)
        load_wu(2)

        query_codes = [held("query_codes%d" % h, [P, S2], U32) for h in range(HALVES)]
        query_scale = held("query_scale", [P, S2], U8)

        def gather_queries(h):
            nc.vector.tensor_copy(query_codes[h][:], query_table[h][:].bitcast(U32).indirect(query_list[:]))

        key_scale_listed = held("key_scale_listed", [P, S], U8)
        key_scale = held("key_scale", [P, PACK, S // PACK], U8)
        key_codes = {}

        def entries(a):
            return key_list[:, a * PASS // 16 : (a + 1) * PASS // 16]

        def gather_key_scales():
            nc.vector.tensor_copy(key_scale_listed[:], key_scale_table[:].indirect(key_list[:]))

        def order_key_scales():
            nc.vector.tensor_copy(key_scale[:], key_scale_listed[:].rearrange("p (m t) -> p t m", t=PACK))

        def gather_keys(h, a):
            key_codes[h, a] = held("key_codes%d_%d" % (h, a), [P, PACK, P], U32)
            nc.vector.tensor_copy(
                key_codes[h, a][:].rearrange("p t m -> p m t"), key_table[h][:].bitcast(U32).indirect(entries(a))
            )

        ROWS = PASSES * PACK
        parts = held("parts", [P, ROWS, 2, 3], F32)
        logs = held("logs", [P, ROWS, 2, 3], F32)
        bias = held("bias", [P, HALVES, ROWS], F32)

        def split_factors():
            given = factors[:, :, :ROWS].rearrange("p s c -> p c s")
            nc.vector.tensor_scalar(parts[:, :, :, 0], given, 1.0 / LN_EDGE, LN_EDGE, ALU.max, ALU.min)
            nc.vector.tensor_scalar(parts[:, :, :, 1], given, 1.0 / LN_EDGE, 1.0, ALU.mult, ALU.max)
            nc.vector.tensor_scalar(parts[:, :, :, 2], given, LN_EDGE, 1.0, ALU.mult, ALU.min)

        def sum_logs():
            for h in range(HALVES):
                for c in range(ROWS):
                    nc.scalar.activation(
                        logs[:, c, : h + 1, :], parts[:, c, : h + 1, :], ACT.Ln, accum_out=bias[:, h, c : c + 1]
                    )

        terms_exp = [[held("exp%d_%d" % (h, a), [P, PACK, S2], F32) for a in range(PASSES)] for h in range(HALVES)]

        banks = [score_banks.tile([P, S2], F32, name="bank%d" % t) for t in range(PACK)]

        def scores(h, a):
            for t in range(PACK):
                bank = banks[t]
                nc.tensor.matmul_mx(
                    out=bank[:],
                    lhsT=key_codes[h, a][:, t, :].bitcast(FP8X4),
                    lhsT_scale=key_scale[KEY_ROW[h] :, t, P * a : P * (a + 1)],
                    rhs=query_codes[h][:].bitcast(FP8X4),
                    rhs_scale=query_scale[QUERY_ROW[h] :, :],
                    start=True,
                    stop=True,
                )
                c = a * PACK + t
                nc.scalar.activation(terms_exp[h][a][:, t, :], bank[:], ACT.Exp, bias=bias[:, h, c : c + 1])

        z_woven = [held("z_woven%d" % a, [P, S2 * PACK], BF16) for a in range(PASSES)]
        z_codes = [held("z_codes%d" % a, [P, S2], U32) for a in range(PASSES)]
        z_scale = [held("z_scale%d" % a, [P, S2], U8) for a in range(PASSES)]
        wu_woven = [held("wu_woven%d" % a, [P, N * PACK], BF16) for a in range(PASSES)]
        wu_codes = [held("wu_codes%d" % a, [P, N], U32) for a in range(PASSES)]
        wu_scale = [held("wu_scale%d" % a, [P, N], U8) for a in range(PASSES)]

        def difference(a, cols):
            nc.vector.tensor_tensor(
                woven(z_woven[a][:, PACK * cols.start : PACK * cols.stop]),
                planes(terms_exp[0][a][:, :, cols]),
                planes(terms_exp[1][a][:, :, cols]),
                ALU.subtract,
            )

        def quantise_z(a):
            nc.vector.quantize_mx(out=z_codes[a][:].bitcast(FP8X4), scales=z_scale[a][:], in_=z_woven[a][:])

        def weave_wu(a, copy, cols):
            copy(woven(wu_woven[a][:, PACK * cols.start : PACK * cols.stop]), planes(wu_rows[a][:, :, cols]))

        def quantise_wu(a, cols):
            nc.vector.quantize_mx(
                out=wu_codes[a][:, cols].bitcast(FP8X4),
                scales=wu_scale[a][:, cols],
                in_=wu_woven[a][:, PACK * cols.start : PACK * cols.stop],
            )

        sums = [out_banks.tile([P, S2], F32, name="sum%d" % b) for b in range(BLOCKS)]

        def mix_w4(a, b):
            nc.tensor.matmul_mx(
                out=sums[b][:],
                lhsT=w4_codes[:, a, 2 * P * b : 2 * P * (b + 1)].bitcast(FP4X4),
                lhsT_scale=w4_scale[:, a, P * b : P * (b + 1)],
                rhs=z_codes[a][:].bitcast(FP8X4),
                rhs_scale=z_scale[a][:],
                start=(a == 0),
                stop=False,
            )

        def mix_wu(a, b):
            nc.tensor.matmul_mx(
                out=sums[b][:],
                lhsT=wu_codes[a][:, P * b : P * (b + 1)].bitcast(FP8X4),
                lhsT_scale=wu_scale[a][:, P * b : P * (b + 1)],
                rhs=z_codes[a][:].bitcast(FP8X4),
                rhs_scale=z_scale[a][:],
                start=False,
                stop=(a == PASSES - 1),
            )

        whole = slice(0, N)
        block = [slice(P * b, P * (b + 1)) for b in range(BLOCKS)]
        gather_queries(0)
        split_factors()
        sum_logs()
        nc.vector.tensor_copy(query_scale[:], query_scale_table[:].indirect(query_list[:]))
        gather_key_scales()
        order_key_scales()
        for a in range(PASSES):
            gather_keys(0, a)
        gather_queries(1)
        for a in range(PASSES):
            gather_keys(1, a)
        for h, a in ((0, 0), (0, 1), (1, 0), (1, 1), (0, 2), (1, 2)):
            scores(h, a)
        half = [slice(0, N // 2), slice(N // 2, N)]
        weave_wu(0, nc.vector.tensor_copy, whole)
        difference(0, whole)
        quantise_wu(0, whole)
        quantise_z(0)
        for b in range(BLOCKS):
            mix_w4(0, b)
            mix_wu(0, b)
        difference(1, whole)
        quantise_z(1)
        for b in range(BLOCKS):
            mix_w4(1, b)
        for u in range(2):
            weave_wu(1, nc.scalar.copy, half[u])
            difference(2, half[u])
            quantise_wu(1, half[u])
            mix_wu(1, 2 * u)
            mix_wu(1, 2 * u + 1)
        quantise_z(2)
        for b in range(BLOCKS):
            weave_wu(2, nc.scalar.copy, block[b])
            quantise_wu(2, block[b])
        results = [held("result%d" % b, [P, S2], F32) for b in range(BLOCKS)]
        for b in range(BLOCKS):
            mix_w4(2, b)
            mix_wu(2, b)
            if b % 2 == 0:
                nc.scalar.copy(results[b][:], sums[b][:])
            else:
                nc.vector.tensor_copy(results[b][:], sums[b][:])
            nc.sync.dma_start(out[P * b : P * (b + 1), :], results[b][:])
